import numpy as np
import ml_dtypes


def mxq(x, axis, fmt="e4m3"):
    dtype, down = {"e4m3": (ml_dtypes.float8_e4m3fn, 7), "e5m2": (ml_dtypes.float8_e5m2, 14)}[fmt]
    v = np.moveaxis(np.asarray(x, np.float32).astype(ml_dtypes.bfloat16).astype(np.float64), axis, -1)
    blocks = v.reshape(v.shape[:-1] + (-1, 32))
    amax = np.abs(blocks).max(-1, keepdims=True)
    byte = np.maximum(np.where(amax > 0, np.frexp(amax)[1] - 1 + 127, 0) - down, 1)
    scale = np.exp2(byte - 127.0)
    codes = (blocks / scale).astype(np.float32).astype(dtype).astype(np.float64)
    return np.moveaxis((codes * scale).reshape(v.shape), -1, axis)


WIDE = False


def mx_kscale(k):
    if not WIDE:
        return np.ones(k)
    levels = np.array([10, -10, 5, -5, 0])
    if k % 512:
        return np.exp2(np.random.permutation(np.resize(levels, k // 32))).repeat(32)
    a = np.empty((k // 512, 16))
    for p in range(k // 512):
        a[p, :8] = np.random.permutation(np.resize(levels, 8))
        for g in range(8):
            far = levels[np.abs(levels - a[p, g]) >= 10]
            a[p, g + 8] = far[np.random.randint(len(far))]
    return np.exp2(a.ravel()).repeat(32)


def f64(x):
    return np.asarray(x).astype(np.float64)


def striped(idx):
    return np.tile(idx.reshape(-1, 16).T, (8, 1)).astype(np.uint16)


def unstriped(offs):
    return offs[:16].T.reshape(-1).astype(np.int64)


def pack_weight(w):
    k, n = w.shape
    w = f64(np.asarray(w, np.float32).astype(ml_dtypes.bfloat16)).reshape(k // 32, 32, n)
    amax = np.abs(w).max(1)
    byte = np.clip(np.where(amax > 0, np.frexp(amax)[1] - 1 + 127 - 7, 1), 1, 254)
    scaled = (w * np.exp2(127.0 - byte)[:, None, :]).reshape(k, n).astype(np.float32)
    words = np.ascontiguousarray(scaled.reshape(k // 512, 128, 4, n).transpose(0, 1, 3, 2)).astype(ml_dtypes.float8_e4m3fn).view(np.uint8)
    return words, np.ascontiguousarray(byte.astype(np.uint8).reshape(k // 512, 16, n))


def unpack_weight(words, scales):
    g, p, n, _ = words.shape
    vals = np.ascontiguousarray(words).view(ml_dtypes.float8_e4m3fn).astype(np.float64) * np.repeat(np.exp2(scales.astype(np.float64) - 127.0), 8, axis=1)[..., None]
    return vals.transpose(0, 1, 3, 2).reshape(g * 512, n)


K, T, S, N, V = 1024, 1024, 512, 128, 256


def setup_inputs():
    n = np.random.standard_normal
    s = mx_kscale(K)[:, None]
    packed_xT = pack_weight(n((K, T)) * s)
    return {
        "x_words": packed_xT[0],
        "x_scales": packed_xT[1],
        "w1": (n((K, N)) / np.sqrt(K) / s).astype(np.float32),
        "offs": striped(np.random.permutation(T)[:S]),
        "pos1": striped(np.random.permutation(S)[:V]),
        "pos2": striped(np.random.permutation(S)[:V]),
        "pos3": striped(np.random.permutation(S)[:V]),
        "pos4": striped(np.random.permutation(S)[:V]),
        "cen": striped(np.random.permutation(S)[:V]),
    }


def reference(x_words, x_scales, w1, offs, pos1, pos2, pos3, pos4, cen):
    xq = unpack_weight(x_words, x_scales)[:, unstriped(offs)]
    y = mxq(f64(w1), 0, "e4m3").T @ xq
    g0 = y[:, unstriped(pos1)]
    g1 = y[:, unstriped(pos2)]
    g2 = y[:, unstriped(pos3)]
    g3 = y[:, unstriped(pos4)]
    lo = np.maximum(np.minimum(g0, g1), np.minimum(g2, g3))
    hi = np.minimum(np.maximum(g0, g1), np.maximum(g2, g3))
    gc = y[:, unstriped(cen)]
    med = np.maximum(np.minimum(lo, hi), np.minimum(np.maximum(lo, hi), gc))
    dev = np.abs(gc - med)
    return np.minimum(med, 0.25 * (g0 + g1 + g2 + g3)) - (0.3 * dev)

@@ -1,0 +1,149 @@
+from contextlib import ExitStack
+
+import concourse.mybir as mybir
+from concourse.masks import make_identity
+
+K, T, S, N, V = 1024, 1024, 512, 128, 256
+FLOPS = 2 * K * N * S
+
+F32 = mybir.dt.float32
+BF16 = mybir.dt.bfloat16
+I32 = mybir.dt.int32
+U32 = mybir.dt.uint32
+U16 = mybir.dt.uint16
+U8 = mybir.dt.uint8
+FP8X4 = mybir.dt.float8_e4m3fn_x4
+ALU = mybir.AluOpType
+ACT = mybir.ActivationFunctionType
+
+P = 128
+PACK = 4
+PASSES = K // (P * PACK)
+LANES = 16
+PIECES = (256, 128, 128)
+TAIL = 2
+
+
+def tile_picked_ymed5f_min_p_kernel(tc, x_words, x_scales, w1, offs, pos1, pos2, pos3, pos4, cen, out):
+    nc = tc.nc
+    with ExitStack() as ctx:
+        keep = ctx.enter_context(tc.tile_pool(name="keep", bufs=1))
+        psum = ctx.enter_context(tc.psum_pool(name="psum", bufs=1))
+
+        def load_list(src, name):
+            lst = keep.tile([P, src.shape[1]], U16, name=name)
+            nc.sync.dma_start(lst[:], src)
+            return lst
+
+        def load_words(o):
+            words = keep.tile([P, T], U32, name="words%d" % o, align_bytes=64)
+            nc.sync.dma_start(words[:].bitcast(I32), x_words[o].rearrange("p n t -> p (n t)").bitcast(I32))
+            return words
+
+        scales = keep.tile([P, T], U8, align_bytes=64)
+        nc.gpsimd.memset(scales[:].bitcast(I32), 0)
+        offs_sb = load_list(offs, "offs_sb")
+        words = [load_words(0)]
+        for q in range(4):
+            nc.sync.dma_start(
+                scales[32 * q : 32 * q + 4 * PASSES, :].bitcast(I32),
+                x_scales[:, 4 * q : 4 * q + 4, :].bitcast(I32),
+            )
+        w_raw = []
+        for o in range(PASSES):
+            raw = keep.tile([P, PACK, N], F32, name="w_raw%d" % o)
+            nc.sync.dma_start(raw[:], w1[o * P * PACK : (o + 1) * P * PACK, :].rearrange("(p j) n -> p j n", j=PACK))
+            w_raw.append(raw)
+        words.append(load_words(1))
+        cen_sb = load_list(cen, "cen_sb")
+        pos_sb = [load_list(src, "pos_sb%d" % i) for i, src in enumerate((pos1, pos2, pos3, pos4))]
+
+        ident = keep.tile([P, P], F32)
+        make_identity(nc, ident[:])
+        warm = keep.tile([P, 1], F32)
+        nc.scalar.activation(warm[:], ident[:, 0:1], ACT.Abs)
+
+        x_codes0 = keep.tile([P, S], U32, align_bytes=64)
+        nc.vector.tensor_copy(x_codes0[:], words[0][:].indirect(offs_sb[:]))
+        x_sc = keep.tile([P, S], U8, align_bytes=64)
+        nc.vector.tensor_copy(x_sc[:], scales[:].indirect(offs_sb[:]))
+
+        w_codes, w_sc = [], []
+        for o in range(PASSES):
+            grouped = keep.tile([P, N, PACK], BF16, name="grouped%d" % o, tag="slot%d" % o, align_bytes=64)
+            nc.scalar.copy(grouped[:], w_raw[o][:].rearrange("p j n -> p n j"))
+            codes = keep.tile([P, N], U32, name="w_codes%d" % o, align_bytes=64)
+            plane = keep.tile([P, N], U8, name="w_sc%d" % o, align_bytes=64)
+            nc.vector.quantize_mx(out=codes[:].bitcast(FP8X4), scales=plane[:], in_=grouped[:].rearrange("p n j -> p (n j)"))
+            w_codes.append(codes)
+            w_sc.append(plane)
+
+        starts = [sum(PIECES[:i]) for i in range(len(PIECES))]
+        banks = [psum.tile([P, n], F32, name="y_bank%d" % i) for i, n in enumerate(PIECES)]
+        for bank, c0, n in zip(banks, starts, PIECES):
+            nc.tensor.matmul_mx(out=bank[:], lhsT=w_codes[0][:].bitcast(FP8X4), lhsT_scale=w_sc[0][:],
+                                rhs=x_codes0[:, c0 : c0 + n].bitcast(FP8X4), rhs_scale=x_sc[:, c0 : c0 + n],
+                                start=True, stop=False)
+        y = keep.tile([P, S], F32)
+        for i, (bank, c0, n) in enumerate(zip(banks, starts, PIECES)):
+            piece = keep.tile([P, n], U32, name="x_codes1_%d" % i, tag="slot%d" % i, align_bytes=64)
+            nc.vector.tensor_copy(piece[:], words[1][:].indirect(offs_sb[:, c0 // LANES : (c0 + n) // LANES]))
+            nc.tensor.matmul_mx(out=bank[:], lhsT=w_codes[1][:].bitcast(FP8X4), lhsT_scale=w_sc[1][:],
+                                rhs=piece[:].bitcast(FP8X4), rhs_scale=x_sc[4:P, c0 : c0 + n],
+                                start=False, stop=True)
+            if i < len(PIECES) - 1:
+                nc.scalar.copy(y[:, c0 : c0 + n], bank[:])
+            else:
+                nc.vector.tensor_copy(y[:, c0 : c0 + n], bank[:])
+
+        halves = [slice(0, P), slice(P, V)]
+        gc = keep.tile([P, V], F32)
+        for h in halves:
+            nc.vector.tensor_copy(gc[:, h], y[:].indirect(cen_sb[:, h.start // LANES : h.stop // LANES]))
+        a_even = keep.tile([P, 2 * V], F32)
+        a_odd = keep.tile([P, 2 * V], F32)
+        a = [a_even[:, :V], a_odd[:, :V], a_even[:, V:], a_odd[:, V:]]
+        for h in halves:
+            nc.vector.tensor_tensor(a[0][:, h], y[:].indirect(pos_sb[0][:, h.start // LANES : h.stop // LANES]), gc[:, h], ALU.subtract)
+        for i in range(1, 4):
+            nc.vector.tensor_tensor(a[i], y[:].indirect(pos_sb[i][:]), gc[:], ALU.subtract)
+
+        sums = [psum.tile([P, P], F32, name="sum_bank%d" % j) for j in range(2)]
+        for i in range(4):
+            for j, h in enumerate(halves):
+                nc.tensor.matmul(sums[j][:], lhsT=a[i][:, h], rhs=ident[:], is_transpose=True, start=(i == 0), stop=(i == 3))
+        mean_t = keep.tile([P, V], F32)
+        mean = psum.tile([P, V], F32, name="mean_bank")
+        for j, h in enumerate(halves):
+            nc.scalar.activation(mean_t[:, h], sums[j][:], ACT.Copy, scale=0.25)
+            nc.tensor.transpose(mean[:, h], mean_t[:, h], ident[:])
+
+        mins = keep.tile([P, 2 * V], F32)
+        maxs = keep.tile([P, 2 * V], F32)
+        nc.vector.tensor_tensor(mins[:], a_even[:], a_odd[:], ALU.min)
+        nc.vector.tensor_tensor(maxs[:], a_even[:], a_odd[:], ALU.max)
+        lo = keep.tile([P, V], F32)
+        hi = keep.tile([P, V], F32)
+        nc.vector.tensor_tensor(lo[:], mins[:, :V], mins[:, V:], ALU.max)
+        nc.vector.tensor_tensor(hi[:], maxs[:, :V], maxs[:, V:], ALU.min)
+
+        parts = [slice(i * V // TAIL, (i + 1) * V // TAIL) for i in range(TAIL)]
+        t = keep.tile([P, V], F32)
+        z = keep.tile([P, V], F32)
+        r = keep.tile([P, V], F32)
+        q = keep.tile([P, V], F32)
+        w = keep.tile([P, V], F32)
+        res = keep.tile([P, V], F32)
+        for c in parts:
+            nc.vector.scalar_tensor_tensor(t[:, c], hi[:, c], 0.0, lo[:, c], ALU.min, ALU.max)
+        for c in parts:
+            nc.vector.scalar_tensor_tensor(z[:, c], hi[:, c], 0.0, t[:, c], ALU.max, ALU.min)
+            nc.scalar.activation(r[:, c], z[:, c], ACT.Abs, scale=0.3)
+        for c in parts:
+            nc.vector.tensor_tensor(q[:, c], mean[:, c], z[:, c], ALU.min)
+        for c in parts:
+            nc.vector.tensor_tensor(w[:, c], q[:, c], gc[:, c], ALU.add)
+        for c in parts:
+            nc.vector.tensor_tensor(res[:, c], w[:, c], r[:, c], ALU.subtract)
+        for h in halves:
+            nc.sync.dma_start(out[:, h], res[:, h])

@@ -21,7 +21,7 @@ PACK = 4
 PASSES = K // (P * PACK)
 LANES = 16
 PIECES = (256, 128, 128)
-TAIL = 2
+TAIL = 4
 
 
 def tile_picked_ymed5f_min_p_kernel(tc, x_words, x_scales, w1, offs, pos1, pos2, pos3, pos4, cen, out):
@@ -68,28 +68,28 @@ def tile_picked_ymed5f_min_p_kernel(tc, x_words, x_scales, w1, offs, pos1, pos2,
         x_sc = keep.tile([P, S], U8, align_bytes=64)
         nc.vector.tensor_copy(x_sc[:], scales[:].indirect(offs_sb[:]))
 
-        w_codes, w_sc = [], []
+        grouped = keep.tile([P, PASSES, N, PACK], BF16, tag="slot", align_bytes=64)
         for o in range(PASSES):
-            grouped = keep.tile([P, N, PACK], BF16, name="grouped%d" % o, tag="slot%d" % o, align_bytes=64)
-            nc.scalar.copy(grouped[:], w_raw[o][:].rearrange("p j n -> p n j"))
-            codes = keep.tile([P, N], U32, name="w_codes%d" % o, align_bytes=64)
-            plane = keep.tile([P, N], U8, name="w_sc%d" % o, align_bytes=64)
-            nc.vector.quantize_mx(out=codes[:].bitcast(FP8X4), scales=plane[:], in_=grouped[:].rearrange("p n j -> p (n j)"))
-            w_codes.append(codes)
-            w_sc.append(plane)
+            nc.scalar.copy(grouped[:, o], w_raw[o][:].rearrange("p j n -> p n j"))
+        codes = keep.tile([P, PASSES * N], U32, align_bytes=64)
+        plane = keep.tile([P, PASSES * N], U8, align_bytes=64)
+        nc.vector.quantize_mx(out=codes[:].bitcast(FP8X4), scales=plane[:], in_=grouped[:].rearrange("p o n j -> p (o n j)"))
+        w_codes = [codes[:, o * N : (o + 1) * N] for o in range(PASSES)]
+        w_sc = [plane[:, o * N : (o + 1) * N] for o in range(PASSES)]
 
         starts = [sum(PIECES[:i]) for i in range(len(PIECES))]
         banks = [psum.tile([P, n], F32, name="y_bank%d" % i) for i, n in enumerate(PIECES)]
         for bank, c0, n in zip(banks, starts, PIECES):
-            nc.tensor.matmul_mx(out=bank[:], lhsT=w_codes[0][:].bitcast(FP8X4), lhsT_scale=w_sc[0][:],
+            nc.tensor.matmul_mx(out=bank[:], lhsT=w_codes[0].bitcast(FP8X4), lhsT_scale=w_sc[0],
                                 rhs=x_codes0[:, c0 : c0 + n].bitcast(FP8X4), rhs_scale=x_sc[:, c0 : c0 + n],
                                 start=True, stop=False)
         y = keep.tile([P, S], F32)
+        x_codes1 = keep.tile([P, S], U32, tag="slot", align_bytes=64)
         for i, (bank, c0, n) in enumerate(zip(banks, starts, PIECES)):
-            piece = keep.tile([P, n], U32, name="x_codes1_%d" % i, tag="slot%d" % i, align_bytes=64)
-            nc.vector.tensor_copy(piece[:], words[1][:].indirect(offs_sb[:, c0 // LANES : (c0 + n) // LANES]))
-            nc.tensor.matmul_mx(out=bank[:], lhsT=w_codes[1][:].bitcast(FP8X4), lhsT_scale=w_sc[1][:],
-                                rhs=piece[:].bitcast(FP8X4), rhs_scale=x_sc[4:P, c0 : c0 + n],
+            piece = x_codes1[:, c0 : c0 + n]
+            nc.vector.tensor_copy(piece, words[1][:].indirect(offs_sb[:, c0 // LANES : (c0 + n) // LANES]))
+            nc.tensor.matmul_mx(out=bank[:], lhsT=w_codes[1].bitcast(FP8X4), lhsT_scale=w_sc[1],
+                                rhs=piece.bitcast(FP8X4), rhs_scale=x_sc[4:P, c0 : c0 + n],
                                 start=False, stop=True)
             if i < len(PIECES) - 1:
                 nc.scalar.copy(y[:, c0 : c0 + n], bank[:])
@@ -97,16 +97,15 @@ def tile_picked_ymed5f_min_p_kernel(tc, x_words, x_scales, w1, offs, pos1, pos2,
                 nc.vector.tensor_copy(y[:, c0 : c0 + n], bank[:])
 
         halves = [slice(0, P), slice(P, V)]
-        gc = keep.tile([P, V], F32)
+        names = ("gc", "a0", "a1", "a2", "a3", "min01", "max01", "min23", "max23", "lo", "hi", "t", "z", "r", "q", "u", "res")
+        gc, a0, a1, a2, a3, min01, max01, min23, max23, lo, hi, t, z, r, q, u, res = [keep.tile([P, V], F32, name=nm) for nm in names]
+        a = [a0, a1, a2, a3]
         for h in halves:
             nc.vector.tensor_copy(gc[:, h], y[:].indirect(cen_sb[:, h.start // LANES : h.stop // LANES]))
-        a_even = keep.tile([P, 2 * V], F32)
-        a_odd = keep.tile([P, 2 * V], F32)
-        a = [a_even[:, :V], a_odd[:, :V], a_even[:, V:], a_odd[:, V:]]
         for h in halves:
-            nc.vector.tensor_tensor(a[0][:, h], y[:].indirect(pos_sb[0][:, h.start // LANES : h.stop // LANES]), gc[:, h], ALU.subtract)
+            nc.vector.tensor_tensor(a0[:, h], y[:].indirect(pos_sb[0][:, h.start // LANES : h.stop // LANES]), gc[:, h], ALU.subtract)
         for i in range(1, 4):
-            nc.vector.tensor_tensor(a[i], y[:].indirect(pos_sb[i][:]), gc[:], ALU.subtract)
+            nc.vector.tensor_tensor(a[i][:], y[:].indirect(pos_sb[i][:]), gc[:], ALU.subtract)
 
         sums = [psum.tile([P, P], F32, name="sum_bank%d" % j) for j in range(2)]
         for i in range(4):
@@ -118,22 +117,14 @@ def tile_picked_ymed5f_min_p_kernel(tc, x_words, x_scales, w1, offs, pos1, pos2,
             nc.scalar.activation(mean_t[:, h], sums[j][:], ACT.Copy, scale=0.25)
             nc.tensor.transpose(mean[:, h], mean_t[:, h], ident[:])
 
-        mins = keep.tile([P, 2 * V], F32)
-        maxs = keep.tile([P, 2 * V], F32)
-        nc.vector.tensor_tensor(mins[:], a_even[:], a_odd[:], ALU.min)
-        nc.vector.tensor_tensor(maxs[:], a_even[:], a_odd[:], ALU.max)
-        lo = keep.tile([P, V], F32)
-        hi = keep.tile([P, V], F32)
-        nc.vector.tensor_tensor(lo[:], mins[:, :V], mins[:, V:], ALU.max)
-        nc.vector.tensor_tensor(hi[:], maxs[:, :V], maxs[:, V:], ALU.min)
-
-        parts = [slice(i * V // TAIL, (i + 1) * V // TAIL) for i in range(TAIL)]
-        t = keep.tile([P, V], F32)
-        z = keep.tile([P, V], F32)
-        r = keep.tile([P, V], F32)
-        q = keep.tile([P, V], F32)
-        w = keep.tile([P, V], F32)
-        res = keep.tile([P, V], F32)
+        nc.vector.tensor_tensor(max01[:], a0[:], a1[:], ALU.max)
+        nc.vector.tensor_tensor(min01[:], a0[:], a1[:], ALU.min)
+        nc.vector.tensor_tensor(max23[:], a2[:], a3[:], ALU.max)
+        nc.vector.tensor_tensor(min23[:], a2[:], a3[:], ALU.min)
+        nc.vector.tensor_tensor(hi[:], max01[:], max23[:], ALU.min)
+        parts = [slice(a, b) for a, b in zip((0, 96, 176, 256), (0, 96, 176, 256)[1:])]
+        for c in parts:
+            nc.vector.tensor_tensor(lo[:, c], min01[:, c], min23[:, c], ALU.max)
         for c in parts:
             nc.vector.scalar_tensor_tensor(t[:, c], hi[:, c], 0.0, lo[:, c], ALU.min, ALU.max)
         for c in parts:
@@ -142,8 +133,8 @@ def tile_picked_ymed5f_min_p_kernel(tc, x_words, x_scales, w1, offs, pos1, pos2,
         for c in parts:
             nc.vector.tensor_tensor(q[:, c], mean[:, c], z[:, c], ALU.min)
         for c in parts:
-            nc.vector.tensor_tensor(w[:, c], q[:, c], gc[:, c], ALU.add)
+            nc.vector.tensor_tensor(u[:, c], gc[:, c], r[:, c], ALU.subtract)
         for c in parts:
-            nc.vector.tensor_tensor(res[:, c], w[:, c], r[:, c], ALU.subtract)
-        for h in halves:
-            nc.sync.dma_start(out[:, h], res[:, h])
+            nc.vector.tensor_tensor(res[:, c], q[:, c], u[:, c], ALU.add)
+        nc.sync.dma_start(out[:, :176], res[:, :176])
+        nc.scalar.dma_start(out[:, 176:], res[:, 176:])

@@ -137,4 +137,4 @@ def tile_picked_ymed5f_min_p_kernel(tc, x_words, x_scales, w1, offs, pos1, pos2,
         for c in parts:
             nc.vector.tensor_tensor(res[:, c], q[:, c], u[:, c], ALU.add)
         nc.sync.dma_start(out[:, :176], res[:, :176])
-        nc.scalar.dma_start(out[:, 176:], res[:, 176:])
+        nc.sync.dma_start(out[:, 176:], res[:, 176:])

@@ -55,8 +55,8 @@ def tile_picked_ymed5f_min_p_kernel(tc, x_words, x_scales, w1, offs, pos1, pos2,
             nc.sync.dma_start(raw[:], w1[o * P * PACK : (o + 1) * P * PACK, :].rearrange("(p j) n -> p j n", j=PACK))
             w_raw.append(raw)
         words.append(load_words(1))
-        cen_sb = load_list(cen, "cen_sb")
         pos_sb = [load_list(src, "pos_sb%d" % i) for i, src in enumerate((pos1, pos2, pos3, pos4))]
+        cen_sb = load_list(cen, "cen_sb")
 
         ident = keep.tile([P, P], F32)
         make_identity(nc, ident[:])
@@ -97,44 +97,45 @@ def tile_picked_ymed5f_min_p_kernel(tc, x_words, x_scales, w1, offs, pos1, pos2,
                 nc.vector.tensor_copy(y[:, c0 : c0 + n], bank[:])
 
         halves = [slice(0, P), slice(P, V)]
-        names = ("gc", "a0", "a1", "a2", "a3", "min01", "max01", "min23", "max23", "lo", "hi", "t", "z", "r", "q", "u", "res")
-        gc, a0, a1, a2, a3, min01, max01, min23, max23, lo, hi, t, z, r, q, u, res = [keep.tile([P, V], F32, name=nm) for nm in names]
-        a = [a0, a1, a2, a3]
-        for h in halves:
-            nc.vector.tensor_copy(gc[:, h], y[:].indirect(cen_sb[:, h.start // LANES : h.stop // LANES]))
-        for h in halves:
-            nc.vector.tensor_tensor(a0[:, h], y[:].indirect(pos_sb[0][:, h.start // LANES : h.stop // LANES]), gc[:, h], ALU.subtract)
-        for i in range(1, 4):
-            nc.vector.tensor_tensor(a[i][:], y[:].indirect(pos_sb[i][:]), gc[:], ALU.subtract)
+        g_even = keep.tile([P, 2 * V], F32)
+        g_odd = keep.tile([P, 2 * V], F32)
+        g = [g_even[:, :V], g_odd[:, :V], g_even[:, V:], g_odd[:, V:]]
+        for i in range(4):
+            nc.vector.tensor_copy(g[i], y[:].indirect(pos_sb[i][:]))
+        gc = keep.tile([P, V], F32)
+        nc.vector.tensor_copy(gc[:], y[:].indirect(cen_sb[:]))
 
         sums = [psum.tile([P, P], F32, name="sum_bank%d" % j) for j in range(2)]
         for i in range(4):
             for j, h in enumerate(halves):
-                nc.tensor.matmul(sums[j][:], lhsT=a[i][:, h], rhs=ident[:], is_transpose=True, start=(i == 0), stop=(i == 3))
+                nc.tensor.matmul(sums[j][:], lhsT=g[i][:, h], rhs=ident[:], is_transpose=True, start=(i == 0), stop=(i == 3))
         mean_t = keep.tile([P, V], F32)
         mean = psum.tile([P, V], F32, name="mean_bank")
         for j, h in enumerate(halves):
             nc.scalar.activation(mean_t[:, h], sums[j][:], ACT.Copy, scale=0.25)
             nc.tensor.transpose(mean[:, h], mean_t[:, h], ident[:])
 
-        nc.vector.tensor_tensor(max01[:], a0[:], a1[:], ALU.max)
-        nc.vector.tensor_tensor(min01[:], a0[:], a1[:], ALU.min)
-        nc.vector.tensor_tensor(max23[:], a2[:], a3[:], ALU.max)
-        nc.vector.tensor_tensor(min23[:], a2[:], a3[:], ALU.min)
-        nc.vector.tensor_tensor(hi[:], max01[:], max23[:], ALU.min)
-        parts = [slice(a, b) for a, b in zip((0, 96, 176, 256), (0, 96, 176, 256)[1:])]
+        names = ("lo", "hi", "low", "up", "t", "med", "e", "r", "q", "res")
+        lo, hi, low, up, t, med, e, r, q, res = [keep.tile([P, V], F32, name=nm) for nm in names]
+        mins = keep.tile([P, 2 * V], F32)
+        maxs = keep.tile([P, 2 * V], F32)
+        nc.vector.tensor_tensor(maxs[:], g_even[:], g_odd[:], ALU.max)
+        nc.vector.tensor_tensor(mins[:], g_even[:], g_odd[:], ALU.min)
+        nc.vector.tensor_tensor(hi[:], maxs[:, :V], maxs[:, V:], ALU.min)
+        nc.vector.tensor_tensor(lo[:], mins[:, :V], mins[:, V:], ALU.max)
+        nc.vector.tensor_tensor(low[:], hi[:], gc[:], ALU.min)
+        nc.vector.tensor_tensor(up[:], hi[:], gc[:], ALU.max)
+        parts = [slice(0, 96), slice(96, 176), slice(176, 256)]
         for c in parts:
-            nc.vector.tensor_tensor(lo[:, c], min01[:, c], min23[:, c], ALU.max)
+            nc.vector.tensor_tensor(t[:, c], lo[:, c], low[:, c], ALU.max)
         for c in parts:
-            nc.vector.scalar_tensor_tensor(t[:, c], hi[:, c], 0.0, lo[:, c], ALU.min, ALU.max)
+            nc.vector.tensor_tensor(med[:, c], t[:, c], up[:, c], ALU.min)
         for c in parts:
-            nc.vector.scalar_tensor_tensor(z[:, c], hi[:, c], 0.0, t[:, c], ALU.max, ALU.min)
-            nc.scalar.activation(r[:, c], z[:, c], ACT.Abs, scale=0.3)
+            nc.vector.tensor_tensor(e[:, c], gc[:, c], med[:, c], ALU.subtract)
+            nc.scalar.activation(r[:, c], e[:, c], ACT.Abs, scale=0.3)
         for c in parts:
-            nc.vector.tensor_tensor(q[:, c], mean[:, c], z[:, c], ALU.min)
+            nc.vector.tensor_tensor(q[:, c], mean[:, c], med[:, c], ALU.min)
         for c in parts:
-            nc.vector.tensor_tensor(u[:, c], gc[:, c], r[:, c], ALU.subtract)
-        for c in parts:
-            nc.vector.tensor_tensor(res[:, c], q[:, c], u[:, c], ALU.add)
+            nc.vector.tensor_tensor(res[:, c], q[:, c], r[:, c], ALU.subtract)
         nc.sync.dma_start(out[:, :176], res[:, :176])
         nc.sync.dma_start(out[:, 176:], res[:, 176:])

@@ -18,10 +18,14 @@ ACT = mybir.ActivationFunctionType
 
 P = 128
 PACK = 4
-PASSES = K // (P * PACK)
+K_PASS = P * PACK
+PASSES = K // K_PASS
+QUADRANT = 32
+SCALE_ROWS = 4
 LANES = 16
+NEIGHBOURS = 4
 PIECES = (256, 128, 128)
-TAIL = 4
+PART_BORDERS = (0, 96, 176, 256)
 
 
 def tile_picked_ymed5f_min_p_kernel(tc, x_words, x_scales, w1, offs, pos1, pos2, pos3, pos4, cen, out):
@@ -36,23 +40,23 @@ def tile_picked_ymed5f_min_p_kernel(tc, x_words, x_scales, w1, offs, pos1, pos2,
             return lst
 
         def load_words(o):
-            words = keep.tile([P, T], U32, name="words%d" % o, align_bytes=64)
-            nc.sync.dma_start(words[:].bitcast(I32), x_words[o].rearrange("p n t -> p (n t)").bitcast(I32))
-            return words
+            tile = keep.tile([P, T], U32, name="words%d" % o, align_bytes=64)
+            nc.sync.dma_start(tile[:].bitcast(I32), x_words[o].rearrange("p n t -> p (n t)").bitcast(I32))
+            return tile
 
         scales = keep.tile([P, T], U8, align_bytes=64)
         nc.gpsimd.memset(scales[:].bitcast(I32), 0)
         offs_sb = load_list(offs, "offs_sb")
         words = [load_words(0)]
-        for q in range(4):
+        for quad in range(P // QUADRANT):
             nc.sync.dma_start(
-                scales[32 * q : 32 * q + 4 * PASSES, :].bitcast(I32),
-                x_scales[:, 4 * q : 4 * q + 4, :].bitcast(I32),
+                scales[QUADRANT * quad : QUADRANT * quad + SCALE_ROWS * PASSES, :].bitcast(I32),
+                x_scales[:, SCALE_ROWS * quad : SCALE_ROWS * (quad + 1), :].bitcast(I32),
             )
         w_raw = []
         for o in range(PASSES):
             raw = keep.tile([P, PACK, N], F32, name="w_raw%d" % o)
-            nc.sync.dma_start(raw[:], w1[o * P * PACK : (o + 1) * P * PACK, :].rearrange("(p j) n -> p j n", j=PACK))
+            nc.sync.dma_start(raw[:], w1[o * K_PASS : (o + 1) * K_PASS, :].rearrange("(p t) n -> p t n", t=PACK))
             w_raw.append(raw)
         words.append(load_words(1))
         pos_sb = [load_list(src, "pos_sb%d" % i) for i, src in enumerate((pos1, pos2, pos3, pos4))]
@@ -60,8 +64,6 @@ def tile_picked_ymed5f_min_p_kernel(tc, x_words, x_scales, w1, offs, pos1, pos2,
 
         ident = keep.tile([P, P], F32)
         make_identity(nc, ident[:])
-        warm = keep.tile([P, 1], F32)
-        nc.scalar.activation(warm[:], ident[:, 0:1], ACT.Abs)
 
         x_codes0 = keep.tile([P, S], U32, align_bytes=64)
         nc.vector.tensor_copy(x_codes0[:], words[0][:].indirect(offs_sb[:]))
@@ -70,72 +72,79 @@ def tile_picked_ymed5f_min_p_kernel(tc, x_words, x_scales, w1, offs, pos1, pos2,
 
         grouped = keep.tile([P, PASSES, N, PACK], BF16, tag="slot", align_bytes=64)
         for o in range(PASSES):
-            nc.scalar.copy(grouped[:, o], w_raw[o][:].rearrange("p j n -> p n j"))
+            nc.scalar.copy(grouped[:, o], w_raw[o][:].rearrange("p t n -> p n t"))
         codes = keep.tile([P, PASSES * N], U32, align_bytes=64)
         plane = keep.tile([P, PASSES * N], U8, align_bytes=64)
-        nc.vector.quantize_mx(out=codes[:].bitcast(FP8X4), scales=plane[:], in_=grouped[:].rearrange("p o n j -> p (o n j)"))
-        w_codes = [codes[:, o * N : (o + 1) * N] for o in range(PASSES)]
+        nc.vector.quantize_mx(out=codes[:].bitcast(FP8X4), scales=plane[:], in_=grouped[:].rearrange("p o n t -> p (o n t)"))
+        w_codes = [codes[:, o * N : (o + 1) * N].bitcast(FP8X4) for o in range(PASSES)]
         w_sc = [plane[:, o * N : (o + 1) * N] for o in range(PASSES)]
 
-        starts = [sum(PIECES[:i]) for i in range(len(PIECES))]
+        pieces = [slice(sum(PIECES[:i]), sum(PIECES[: i + 1])) for i in range(len(PIECES))]
         banks = [psum.tile([P, n], F32, name="y_bank%d" % i) for i, n in enumerate(PIECES)]
-        for bank, c0, n in zip(banks, starts, PIECES):
-            nc.tensor.matmul_mx(out=bank[:], lhsT=w_codes[0].bitcast(FP8X4), lhsT_scale=w_sc[0],
-                                rhs=x_codes0[:, c0 : c0 + n].bitcast(FP8X4), rhs_scale=x_sc[:, c0 : c0 + n],
-                                start=True, stop=False)
+        for bank, cols in zip(banks, pieces):
+            nc.tensor.matmul_mx(
+                out=bank[:], lhsT=w_codes[0], lhsT_scale=w_sc[0],
+                rhs=x_codes0[:, cols].bitcast(FP8X4), rhs_scale=x_sc[:, cols], start=True, stop=False,
+            )
         y = keep.tile([P, S], F32)
         x_codes1 = keep.tile([P, S], U32, tag="slot", align_bytes=64)
-        for i, (bank, c0, n) in enumerate(zip(banks, starts, PIECES)):
-            piece = x_codes1[:, c0 : c0 + n]
-            nc.vector.tensor_copy(piece, words[1][:].indirect(offs_sb[:, c0 // LANES : (c0 + n) // LANES]))
-            nc.tensor.matmul_mx(out=bank[:], lhsT=w_codes[1].bitcast(FP8X4), lhsT_scale=w_sc[1],
-                                rhs=piece.bitcast(FP8X4), rhs_scale=x_sc[4:P, c0 : c0 + n],
-                                start=False, stop=True)
-            if i < len(PIECES) - 1:
-                nc.scalar.copy(y[:, c0 : c0 + n], bank[:])
+        for bank, cols in zip(banks, pieces):
+            entries = offs_sb[:, cols.start // LANES : cols.stop // LANES]
+            nc.vector.tensor_copy(x_codes1[:, cols], words[1][:].indirect(entries))
+            nc.tensor.matmul_mx(
+                out=bank[:], lhsT=w_codes[1], lhsT_scale=w_sc[1],
+                rhs=x_codes1[:, cols].bitcast(FP8X4), rhs_scale=x_sc[SCALE_ROWS:P, cols], start=False, stop=True,
+            )
+            if cols.stop < S:
+                nc.scalar.copy(y[:, cols], bank[:])
             else:
-                nc.vector.tensor_copy(y[:, c0 : c0 + n], bank[:])
+                nc.vector.tensor_copy(y[:, cols], bank[:])
 
-        halves = [slice(0, P), slice(P, V)]
         g_even = keep.tile([P, 2 * V], F32)
         g_odd = keep.tile([P, 2 * V], F32)
         g = [g_even[:, :V], g_odd[:, :V], g_even[:, V:], g_odd[:, V:]]
-        for i in range(4):
+        for i in range(NEIGHBOURS):
             nc.vector.tensor_copy(g[i], y[:].indirect(pos_sb[i][:]))
         gc = keep.tile([P, V], F32)
         nc.vector.tensor_copy(gc[:], y[:].indirect(cen_sb[:]))
 
-        sums = [psum.tile([P, P], F32, name="sum_bank%d" % j) for j in range(2)]
-        for i in range(4):
-            for j, h in enumerate(halves):
-                nc.tensor.matmul(sums[j][:], lhsT=g[i][:, h], rhs=ident[:], is_transpose=True, start=(i == 0), stop=(i == 3))
+        blocks = [slice(b * P, (b + 1) * P) for b in range(V // P)]
+        sums = [psum.tile([P, P], F32, name="sum_bank%d" % b) for b in range(V // P)]
+        for i in range(NEIGHBOURS):
+            for total, block in zip(sums, blocks):
+                nc.tensor.matmul(
+                    total[:], lhsT=g[i][:, block], rhs=ident[:], is_transpose=True,
+                    start=(i == 0), stop=(i == NEIGHBOURS - 1),
+                )
         mean_t = keep.tile([P, V], F32)
         mean = psum.tile([P, V], F32, name="mean_bank")
-        for j, h in enumerate(halves):
-            nc.scalar.activation(mean_t[:, h], sums[j][:], ACT.Copy, scale=0.25)
-            nc.tensor.transpose(mean[:, h], mean_t[:, h], ident[:])
+        for total, block in zip(sums, blocks):
+            nc.scalar.activation(mean_t[:, block], total[:], ACT.Copy, scale=1.0 / NEIGHBOURS)
+            nc.tensor.transpose(mean[:, block], mean_t[:, block], ident[:])
 
-        names = ("lo", "hi", "low", "up", "t", "med", "e", "r", "q", "res")
-        lo, hi, low, up, t, med, e, r, q, res = [keep.tile([P, V], F32, name=nm) for nm in names]
+        names = ("lo", "hi", "floor", "ceil", "raised", "med", "diff", "penalty", "smaller", "res")
+        lo, hi, floor, ceil, raised, med, diff, penalty, smaller, res = [keep.tile([P, V], F32, name=nm) for nm in names]
         mins = keep.tile([P, 2 * V], F32)
         maxs = keep.tile([P, 2 * V], F32)
         nc.vector.tensor_tensor(maxs[:], g_even[:], g_odd[:], ALU.max)
         nc.vector.tensor_tensor(mins[:], g_even[:], g_odd[:], ALU.min)
         nc.vector.tensor_tensor(hi[:], maxs[:, :V], maxs[:, V:], ALU.min)
         nc.vector.tensor_tensor(lo[:], mins[:, :V], mins[:, V:], ALU.max)
-        nc.vector.tensor_tensor(low[:], hi[:], gc[:], ALU.min)
-        nc.vector.tensor_tensor(up[:], hi[:], gc[:], ALU.max)
-        parts = [slice(0, 96), slice(96, 176), slice(176, 256)]
-        for c in parts:
-            nc.vector.tensor_tensor(t[:, c], lo[:, c], low[:, c], ALU.max)
-        for c in parts:
-            nc.vector.tensor_tensor(med[:, c], t[:, c], up[:, c], ALU.min)
-        for c in parts:
-            nc.vector.tensor_tensor(e[:, c], gc[:, c], med[:, c], ALU.subtract)
-            nc.scalar.activation(r[:, c], e[:, c], ACT.Abs, scale=0.3)
-        for c in parts:
-            nc.vector.tensor_tensor(q[:, c], mean[:, c], med[:, c], ALU.min)
-        for c in parts:
-            nc.vector.tensor_tensor(res[:, c], q[:, c], r[:, c], ALU.subtract)
-        nc.sync.dma_start(out[:, :176], res[:, :176])
-        nc.sync.dma_start(out[:, 176:], res[:, 176:])
+        nc.vector.tensor_tensor(floor[:], hi[:], gc[:], ALU.min)
+        nc.vector.tensor_tensor(ceil[:], hi[:], gc[:], ALU.max)
+        parts = [slice(first, end) for first, end in zip(PART_BORDERS, PART_BORDERS[1:])]
+        for part in parts:
+            nc.vector.tensor_tensor(raised[:, part], lo[:, part], floor[:, part], ALU.max)
+        for part in parts:
+            nc.vector.tensor_tensor(med[:, part], raised[:, part], ceil[:, part], ALU.min)
+        for part in parts:
+            nc.vector.tensor_tensor(diff[:, part], gc[:, part], med[:, part], ALU.subtract)
+            nc.scalar.activation(penalty[:, part], diff[:, part], ACT.Abs, scale=0.3)
+        for part in parts:
+            nc.vector.tensor_tensor(smaller[:, part], mean[:, part], med[:, part], ALU.min)
+        for part in parts:
+            nc.vector.tensor_tensor(res[:, part], smaller[:, part], penalty[:, part], ALU.subtract)
+
+        last = parts[-1].start
+        nc.sync.dma_start(out[:, :last], res[:, :last])
+        nc.sync.dma_start(out[:, last:], res[:, last:])

from contextlib import ExitStack

import concourse.mybir as mybir
from concourse.masks import make_identity

K, T, S, N, V = 1024, 1024, 512, 128, 256
FLOPS = 2 * K * N * S

F32 = mybir.dt.float32
BF16 = mybir.dt.bfloat16
I32 = mybir.dt.int32
U32 = mybir.dt.uint32
U16 = mybir.dt.uint16
U8 = mybir.dt.uint8
FP8X4 = mybir.dt.float8_e4m3fn_x4
ALU = mybir.AluOpType
ACT = mybir.ActivationFunctionType

P = 128
PACK = 4
K_PASS = P * PACK
PASSES = K // K_PASS
QUADRANT = 32
SCALE_ROWS = 4
LANES = 16
NEIGHBOURS = 4
PIECES = (256, 128, 128)
PART_BORDERS = (0, 96, 176, 256)


def tile_picked_ymed5f_min_p_kernel(tc, x_words, x_scales, w1, offs, pos1, pos2, pos3, pos4, cen, out):
    nc = tc.nc
    with ExitStack() as ctx:
        keep = ctx.enter_context(tc.tile_pool(name="keep", bufs=1))
        psum = ctx.enter_context(tc.psum_pool(name="psum", bufs=1))

        def load_list(src, name):
            lst = keep.tile([P, src.shape[1]], U16, name=name)
            nc.sync.dma_start(lst[:], src)
            return lst

        def load_words(o):
            tile = keep.tile([P, T], U32, name="words%d" % o, align_bytes=64)
            nc.sync.dma_start(tile[:].bitcast(I32), x_words[o].rearrange("p n t -> p (n t)").bitcast(I32))
            return tile

        scales = keep.tile([P, T], U8, align_bytes=64)
        nc.gpsimd.memset(scales[:].bitcast(I32), 0)
        offs_sb = load_list(offs, "offs_sb")
        words = [load_words(0)]
        for quad in range(P // QUADRANT):
            nc.sync.dma_start(
                scales[QUADRANT * quad : QUADRANT * quad + SCALE_ROWS * PASSES, :].bitcast(I32),
                x_scales[:, SCALE_ROWS * quad : SCALE_ROWS * (quad + 1), :].bitcast(I32),
            )
        w_raw = []
        for o in range(PASSES):
            raw = keep.tile([P, PACK, N], F32, name="w_raw%d" % o)
            nc.sync.dma_start(raw[:], w1[o * K_PASS : (o + 1) * K_PASS, :].rearrange("(p t) n -> p t n", t=PACK))
            w_raw.append(raw)
        words.append(load_words(1))
        pos_sb = [load_list(src, "pos_sb%d" % i) for i, src in enumerate((pos1, pos2, pos3, pos4))]
        cen_sb = load_list(cen, "cen_sb")

        ident = keep.tile([P, P], F32)
        make_identity(nc, ident[:])

        x_codes0 = keep.tile([P, S], U32, align_bytes=64)
        nc.vector.tensor_copy(x_codes0[:], words[0][:].indirect(offs_sb[:]))
        x_sc = keep.tile([P, S], U8, align_bytes=64)
        nc.vector.tensor_copy(x_sc[:], scales[:].indirect(offs_sb[:]))

        grouped = keep.tile([P, PASSES, N, PACK], BF16, tag="slot", align_bytes=64)
        for o in range(PASSES):
            nc.scalar.copy(grouped[:, o], w_raw[o][:].rearrange("p t n -> p n t"))
        codes = keep.tile([P, PASSES * N], U32, align_bytes=64)
        plane = keep.tile([P, PASSES * N], U8, align_bytes=64)
        nc.vector.quantize_mx(out=codes[:].bitcast(FP8X4), scales=plane[:], in_=grouped[:].rearrange("p o n t -> p (o n t)"))
        w_codes = [codes[:, o * N : (o + 1) * N].bitcast(FP8X4) for o in range(PASSES)]
        w_sc = [plane[:, o * N : (o + 1) * N] for o in range(PASSES)]

        pieces = [slice(sum(PIECES[:i]), sum(PIECES[: i + 1])) for i in range(len(PIECES))]
        banks = [psum.tile([P, n], F32, name="y_bank%d" % i) for i, n in enumerate(PIECES)]
        for bank, cols in zip(banks, pieces):
            nc.tensor.matmul_mx(
                out=bank[:], lhsT=w_codes[0], lhsT_scale=w_sc[0],
                rhs=x_codes0[:, cols].bitcast(FP8X4), rhs_scale=x_sc[:, cols], start=True, stop=False,
            )
        y = keep.tile([P, S], F32)
        x_codes1 = keep.tile([P, S], U32, tag="slot", align_bytes=64)
        for bank, cols in zip(banks, pieces):
            entries = offs_sb[:, cols.start // LANES : cols.stop // LANES]
            nc.vector.tensor_copy(x_codes1[:, cols], words[1][:].indirect(entries))
            nc.tensor.matmul_mx(
                out=bank[:], lhsT=w_codes[1], lhsT_scale=w_sc[1],
                rhs=x_codes1[:, cols].bitcast(FP8X4), rhs_scale=x_sc[SCALE_ROWS:P, cols], start=False, stop=True,
            )
            if cols.stop < S:
                nc.scalar.copy(y[:, cols], bank[:])
            else:
                nc.vector.tensor_copy(y[:, cols], bank[:])

        g_even = keep.tile([P, 2 * V], F32)
        g_odd = keep.tile([P, 2 * V], F32)
        g = [g_even[:, :V], g_odd[:, :V], g_even[:, V:], g_odd[:, V:]]
        for i in range(NEIGHBOURS):
            nc.vector.tensor_copy(g[i], y[:].indirect(pos_sb[i][:]))
        gc = keep.tile([P, V], F32)
        nc.vector.tensor_copy(gc[:], y[:].indirect(cen_sb[:]))

        blocks = [slice(b * P, (b + 1) * P) for b in range(V // P)]
        sums = [psum.tile([P, P], F32, name="sum_bank%d" % b) for b in range(V // P)]
        for i in range(NEIGHBOURS):
            for total, block in zip(sums, blocks):
                nc.tensor.matmul(
                    total[:], lhsT=g[i][:, block], rhs=ident[:], is_transpose=True,
                    start=(i == 0), stop=(i == NEIGHBOURS - 1),
                )
        mean_t = keep.tile([P, V], F32)
        mean = psum.tile([P, V], F32, name="mean_bank")
        for total, block in zip(sums, blocks):
            nc.scalar.activation(mean_t[:, block], total[:], ACT.Copy, scale=1.0 / NEIGHBOURS)
            nc.tensor.transpose(mean[:, block], mean_t[:, block], ident[:])

        names = ("lo", "hi", "floor", "ceil", "raised", "med", "diff", "penalty", "smaller", "res")
        lo, hi, floor, ceil, raised, med, diff, penalty, smaller, res = [keep.tile([P, V], F32, name=nm) for nm in names]
        mins = keep.tile([P, 2 * V], F32)
        maxs = keep.tile([P, 2 * V], F32)
        nc.vector.tensor_tensor(maxs[:], g_even[:], g_odd[:], ALU.max)
        nc.vector.tensor_tensor(mins[:], g_even[:], g_odd[:], ALU.min)
        nc.vector.tensor_tensor(hi[:], maxs[:, :V], maxs[:, V:], ALU.min)
        nc.vector.tensor_tensor(lo[:], mins[:, :V], mins[:, V:], ALU.max)
        nc.vector.tensor_tensor(floor[:], hi[:], gc[:], ALU.min)
        nc.vector.tensor_tensor(ceil[:], hi[:], gc[:], ALU.max)
        parts = [slice(first, end) for first, end in zip(PART_BORDERS, PART_BORDERS[1:])]
        for part in parts:
            nc.vector.tensor_tensor(raised[:, part], lo[:, part], floor[:, part], ALU.max)
        for part in parts:
            nc.vector.tensor_tensor(med[:, part], raised[:, part], ceil[:, part], ALU.min)
        for part in parts:
            nc.vector.tensor_tensor(diff[:, part], gc[:, part], med[:, part], ALU.subtract)
            nc.scalar.activation(penalty[:, part], diff[:, part], ACT.Abs, scale=0.3)
        for part in parts:
            nc.vector.tensor_tensor(smaller[:, part], mean[:, part], med[:, part], ALU.min)
        for part in parts:
            nc.vector.tensor_tensor(res[:, part], smaller[:, part], penalty[:, part], ALU.subtract)

        last = parts[-1].start
        nc.sync.dma_start(out[:, :last], res[:, :last])
        nc.sync.dma_start(out[:, last:], res[:, last:])
